import numpy as np
import ml_dtypes


def mxq(x, axis, fmt="e4m3"):
    dtype, down = {"e4m3": (ml_dtypes.float8_e4m3fn, 7), "e5m2": (ml_dtypes.float8_e5m2, 14)}[fmt]
    v = np.moveaxis(np.asarray(x, np.float32).astype(ml_dtypes.bfloat16).astype(np.float64), axis, -1)
    blocks = v.reshape(v.shape[:-1] + (-1, 32))
    amax = np.abs(blocks).max(-1, keepdims=True)
    byte = np.maximum(np.where(amax > 0, np.frexp(amax)[1] - 1 + 127, 0) - down, 1)
    scale = np.exp2(byte - 127.0)
    codes = (blocks / scale).astype(np.float32).astype(dtype).astype(np.float64)
    return np.moveaxis((codes * scale).reshape(v.shape), -1, axis)


WIDE = False


def mx_kscale(k):
    if not WIDE:
        return np.ones(k)
    levels = np.array([30, -30])
    if k % 512:
        return np.exp2(np.random.permutation(np.resize(levels, k // 32))).repeat(32)
    a = np.empty((k // 512, 16))
    for p in range(k // 512):
        a[p, :8] = np.random.permutation(np.resize(levels, 8))
        for g in range(8):
            far = levels[np.abs(levels - a[p, g]) >= 10]
            a[p, g + 8] = far[np.random.randint(len(far))]
    return np.exp2(a.ravel()).repeat(32)


def f64(x):
    return np.asarray(x).astype(np.float64)


def striped(idx):
    return np.tile(np.asarray(idx).reshape(-1, 16).T, (8, 1)).astype(np.uint16)


def unstriped(offs):
    return offs[:16].T.reshape(-1).astype(np.int64)


E2M1 = np.array([0.0, 0.5, 1.0, 1.5, 2.0, 3.0, 4.0, 6.0, -0.0, -0.5, -1.0, -1.5, -2.0, -3.0, -4.0, -6.0])


def pack_weight(w, fmt):
    k, n = w.shape
    w = f64(np.asarray(w, np.float32).astype(ml_dtypes.bfloat16)).reshape(k // 32, 32, n)
    amax = np.abs(w).max(1)
    if fmt in ("e4m3", "e5m2"):
        byte = np.frexp(amax)[1] - 1 + 127 - (7 if fmt == "e4m3" else 14)
    else:
        mant, ex = np.frexp(amax / 6.0)
        byte = np.where(mant > 0.5, ex, ex - 1) + 127
    byte = np.clip(np.where(amax > 0, byte, 1), 1, 254)
    scaled = (w * np.exp2(127.0 - byte)[:, None, :]).reshape(k, n).astype(np.float32)
    by_word = np.ascontiguousarray(scaled.reshape(k // 512, 128, 4, n).transpose(0, 1, 3, 2))
    if fmt in ("e4m3", "e5m2"):
        words = by_word.astype(ml_dtypes.float8_e4m3fn if fmt == "e4m3" else ml_dtypes.float8_e5m2).view(np.uint8)
    else:
        c = by_word.astype(ml_dtypes.float4_e2m1fn).view(np.uint8) & 0xF
        words = (c[..., 0::2] | (c[..., 1::2] << 4)).reshape(k // 512, 128, 2 * n)
    return np.ascontiguousarray(words), np.ascontiguousarray(byte.astype(np.uint8).reshape(k // 512, 16, n))


def unpack_weight(words, scales, fmt):
    g, _, n = scales.shape
    words = np.ascontiguousarray(words).reshape(g, 128, n, -1)
    if fmt in ("e4m3", "e5m2"):
        vals = words.view(ml_dtypes.float8_e4m3fn if fmt == "e4m3" else ml_dtypes.float8_e5m2).astype(np.float64)
    else:
        nib = np.empty((g, 128, n, 4), np.uint8)
        nib[..., 0::2] = words & 0xF
        nib[..., 1::2] = words >> 4
        vals = E2M1[nib]
    vals = vals * np.repeat(np.exp2(scales.astype(np.float64) - 127.0), 8, axis=1)[..., None]
    return vals.transpose(0, 1, 3, 2).reshape(g * 512, n)


K, F, T, Z, J, R, N = 512, 512, 1024, 1024, 256, 512, 256


def setup_inputs():
    n = np.random.standard_normal
    idx = np.random.permutation(T)[:J]
    idx2 = np.random.permutation(Z)[:J]
    idx3 = np.random.permutation(J)[:J]
    fk = mx_kscale(K)
    fr = mx_kscale(R)
    ff = mx_kscale(F)
    xtp = pack_weight(n((K, T)) / fk[:, None], "e2m1")
    wp = pack_weight(n((K, R)) * 1 / np.sqrt(K) * fk[:, None] * fr, "e4m3")
    xop = pack_weight(n((F, Z)) / ff[:, None], "e4m3")
    w2p = pack_weight(n((F, R)) * 1 / np.sqrt(F) * ff[:, None] * fr, "e2m1")
    wbp = pack_weight(n((R, N)) * 1 / np.sqrt(R) / fr[:, None], "e2m1")
    wcp = pack_weight(n((R, N)) * 1 / np.sqrt(R) / fr[:, None], "e5m2")
    return {
        "xt_words": xtp[0],
        "xt_scales": xtp[1],
        "w_words": wp[0],
        "w_scales": wp[1],
        "xo_words": xop[0],
        "xo_scales": xop[1],
        "w2_words": w2p[0],
        "w2_scales": w2p[1],
        "wb_words": wbp[0],
        "wb_scales": wbp[1],
        "wc_words": wcp[0],
        "wc_scales": wcp[1],
        "so": (np.random.uniform(0.5, 1.6, (N, 1))).astype(np.float32),
        "offs": striped(idx),
        "offs2": striped(idx2),
        "offs3": striped(idx3),
    }


def reference(xt_words, xt_scales, w_words, w_scales, xo_words, xo_scales, w2_words, w2_scales, wb_words, wb_scales, wc_words, wc_scales, so, offs, offs2, offs3):
    idx = unstriped(offs)
    idx2 = unstriped(offs2)
    idx3 = unstriped(offs3)
    xtu = unpack_weight(xt_words, xt_scales, "e2m1")
    wu = unpack_weight(w_words, w_scales, "e4m3")
    xou = unpack_weight(xo_words, xo_scales, "e4m3")
    w2u = unpack_weight(w2_words, w2_scales, "e2m1")
    wbu = unpack_weight(wb_words, wb_scales, "e2m1")
    wcu = unpack_weight(wc_words, wc_scales, "e5m2")
    xtidxg = xtu[:, idx]
    a = wu.T @ xtidxg
    xoidx2g = xou[:, idx2]
    b = w2u.T @ xoidx2g
    hid = np.abs(a - b)
    hidq = mxq(hid, 0, "e5m2")
    p = wbu.T @ hidq
    q = wcu.T @ hidq
    m0 = np.maximum(p, q)
    y = m0 - m0[:, idx3] * f64(so)
    return y

@@ -1,0 +1,210 @@
+from contextlib import ExitStack
+
+import concourse.mybir as mybir
+
+FLOPS = 402653184
+
+F32 = mybir.dt.float32
+BF16 = mybir.dt.bfloat16
+I32 = mybir.dt.int32
+U32 = mybir.dt.uint32
+U16 = mybir.dt.uint16
+U8 = mybir.dt.uint8
+E4M3 = mybir.dt.float8_e4m3fn_x4
+E5M2 = mybir.dt.float8_e5m2_x4
+E2M1 = mybir.dt.float4_e2m1fn_x4
+ACT = mybir.ActivationFunctionType
+ALU = mybir.AluOpType
+
+P = 128
+PACK = 4
+TABLE = 1024
+J = 256
+R = 512
+N = 256
+HALF = 128
+QUARTER = 64
+LIST_ROWS = 16
+
+
+def tile_list_outcomeneighbours_twotab_kernel(
+    tc, xt_words, xt_scales, w_words, w_scales, xo_words, xo_scales, w2_words, w2_scales,
+    wb_words, wb_scales, wc_words, wc_scales, so, offs, offs2, offs3, out,
+):
+    nc = tc.nc
+    with ExitStack() as ctx:
+        sb = ctx.enter_context(tc.tile_pool(name="sb", bufs=1))
+        ps = ctx.enter_context(tc.psum_pool(name="ps", bufs=1))
+
+        def tile(name, width, dtype):
+            return sb.tile([P, width], dtype, name=name, align_bytes=64)
+
+        def load_words(queue, dst, src):
+            queue.dma_start(out=dst[:].bitcast(I32), in_=src.bitcast(I32))
+
+        def load_scales(queue, dst, src):
+            for q in range(4):
+                queue.dma_start(
+                    out=dst[32 * q : 32 * q + 4, :].bitcast(I32),
+                    in_=src[0, 4 * q : 4 * q + 4, :].bitcast(I32),
+                )
+
+        def load_scale_pairs(queue, first, src):
+            width = src.shape[2]
+            by_quadrant = src[0].rearrange("(b e r) c -> e r b c", b=2, e=2)
+            for e in range(2):
+                queue.dma_start(
+                    out=planes[32 * e : 32 * e + 4, :, first : first + width].bitcast(I32),
+                    in_=by_quadrant[e].bitcast(I32),
+                )
+
+        def lift_upper_quadrants(width):
+            nc.vector.tensor_copy(
+                out=planes[64:128, 0, 0:width].bitcast(I32), in_=planes[0:64, 1, 0:width].bitcast(I32)
+            )
+
+        def fp8_words(src):
+            return src[0].rearrange("p n t -> p (n t)")
+
+        list1 = sb.tile([P, J // LIST_ROWS], U16, name="list1")
+        list2 = sb.tile([P, J // LIST_ROWS], U16, name="list2")
+        list3 = sb.tile([P, J // LIST_ROWS], U16, name="list3")
+        xt_w, xt_s = tile("xt_w", TABLE, U16), tile("xt_s", TABLE, U8)
+        xo_w, xo_s = tile("xo_w", TABLE, U32), tile("xo_s", TABLE, U8)
+        w_w, w2_w = tile("w_w", R, U32), tile("w2_w", R, U16)
+        planes = sb.tile([P, 2, 2 * R], U8, name="planes", align_bytes=64)
+        so_t = tile("so_t", 2, F32)
+
+        nc.vector.memset(planes[0:64, :, 0:R].bitcast(I32), 0)
+        nc.vector.memset(planes[0:64, :, R : 2 * R].bitcast(I32), 0)
+        nc.vector.memset(xt_s[:].bitcast(I32), 0)
+        nc.vector.memset(xo_s[:].bitcast(I32), 0)
+
+        load_words(nc.gpsimd, w_w, fp8_words(w_words))
+        load_words(nc.gpsimd, xo_w, fp8_words(xo_words))
+        load_words(nc.gpsimd, w2_w, w2_words[0])
+        nc.sync.dma_start(list1[:], offs)
+        load_words(nc.sync, xt_w, xt_words[0])
+        nc.sync.dma_start(list2[:], offs2)
+        load_scale_pairs(nc.sync, 0, w_scales)
+        load_scale_pairs(nc.sync, R, w2_scales)
+        load_scales(nc.sync, xt_s, xt_scales)
+        load_scales(nc.sync, xo_s, xo_scales)
+        nc.sync.dma_start(list3[:], offs3)
+        with nc.allow_non_contiguous_dma(reason="one weight a partition"):
+            nc.gpsimd.dma_start(out=so_t[:], in_=so.rearrange("(t p) o -> p (t o)", p=P))
+
+        def dealt(copy, dst, src):
+            copy(
+                out=dst.rearrange("p (t m) -> p m t", t=PACK),
+                in_=src.rearrange("p (m t) -> p m t", t=PACK),
+            )
+            return dst
+
+        def gathered(name, table, offsets, width, dtype):
+            dst = tile(name, width, dtype)
+            nc.vector.tensor_copy(dst[:], table[:].indirect(offsets))
+            return dst
+
+        def half_of(lst, h):
+            return lst[:, 8 * h : 8 * h + 8]
+
+        lift_upper_quadrants(2 * R)
+        g_xt_w = gathered("g_xt_w", xt_w, list1[:], J, U16)
+        w_wd = dealt(nc.scalar.copy, tile("w_wd", R, U32)[:], w_w[:])
+        w2_wd = dealt(nc.scalar.copy, w_w[:, N : 2 * N].bitcast(U16), w2_w[:])
+        w_sd = dealt(nc.vector.tensor_copy, tile("w_sd", R, U8)[:], planes[:, 0, 0:R])
+        w2_sd = dealt(nc.vector.tensor_copy, tile("w2_sd", R, U8)[:], planes[:, 0, R : 2 * R])
+        g_xo_w = [gathered("g_xo_w%d" % h, xo_w, half_of(list2, h), HALF, U32) for h in range(2)]
+        g_xt_s = [gathered("g_xt_s%d" % h, xt_s, half_of(list1, h), HALF, U8) for h in range(2)]
+        g_xo_s = [gathered("g_xo_s%d" % h, xo_s, half_of(list2, h), HALF, U8) for h in range(2)]
+
+        wc_w, wb_w = w_w[:, 0:N], w2_w[:, 0:N]
+        wb_s, wc_s = planes[:, 0, 0:N], planes[:, 0, N : 2 * N]
+        load_scale_pairs(nc.sync, 0, wb_scales)
+        load_scale_pairs(nc.sync, N, wc_scales)
+        load_words(nc.sync, wc_w, fp8_words(wc_words))
+        load_words(nc.sync, wb_w, wb_words[0])
+
+        a_sb = []
+        for h in range(2):
+            bank = ps.tile([P, PACK, HALF], F32, name="a_ps%d" % h)
+            cols = slice(HALF * h, HALF * (h + 1))
+            for t in range(PACK):
+                rows = slice(P * t, P * (t + 1))
+                nc.tensor.matmul_mx(
+                    out=bank[:, t, :],
+                    lhsT=w_wd[:, rows].bitcast(E4M3), lhsT_scale=w_sd[:, rows],
+                    rhs=g_xt_w[:, cols].bitcast(E2M1), rhs_scale=g_xt_s[h][:],
+                    start=True, stop=True,
+                )
+            a_h = tile("a_sb%d" % h, PACK * HALF, F32)
+            nc.scalar.activation(
+                out=a_h[:].rearrange("p (j t) -> p j t", t=PACK),
+                in_=bank[:].rearrange("p t j -> p j t"),
+                func=ACT.Copy,
+            )
+            a_sb.append(a_h)
+
+        b_ps = []
+        for h in range(2):
+            bank = ps.tile([P, PACK, HALF], F32, name="b_ps%d" % h)
+            for t in range(PACK):
+                rows = slice(P * t, P * (t + 1))
+                nc.tensor.matmul_mx(
+                    out=bank[:, t, :],
+                    lhsT=w2_wd[:, rows].bitcast(E2M1), lhsT_scale=w2_sd[:, rows],
+                    rhs=g_xo_w[h][:].bitcast(E4M3), rhs_scale=g_xo_s[h][:],
+                    start=True, stop=True,
+                )
+            b_ps.append(bank)
+
+        lift_upper_quadrants(2 * N)
+        m0 = [tile("m0_%d" % nh, J, F32) for nh in range(2)]
+        for h in range(2):
+            hid = tile("hid%d" % h, PACK * HALF, BF16)
+            for u in range(2):
+                span = slice(PACK * QUARTER * u, PACK * QUARTER * (u + 1))
+                diff = tile("diff%d%d" % (h, u), PACK * QUARTER, F32)
+                nc.vector.tensor_tensor(
+                    out=diff[:].rearrange("p (j t) -> p j t", t=PACK),
+                    in0=a_sb[h][:, span].rearrange("p (j t) -> p j t", t=PACK),
+                    in1=b_ps[h][:, :, QUARTER * u : QUARTER * (u + 1)].rearrange("p t j -> p j t"),
+                    op=ALU.subtract,
+                )
+                nc.scalar.activation(out=hid[:, span], in_=diff[:], func=ACT.Abs)
+            hid_w, hid_s = tile("hid_w%d" % h, HALF, U32), tile("hid_s%d" % h, HALF, U8)
+            nc.vector.quantize_mx(out=hid_w[:].bitcast(E5M2), scales=hid_s[:], in_=hid[:])
+            for nh in range(2):
+                rows = slice(P * nh, P * (nh + 1))
+                bank = ps.tile([P, 2, HALF], F32, name="pq_ps%d%d" % (h, nh))
+                nc.tensor.matmul_mx(
+                    out=bank[:, 0, :],
+                    lhsT=wb_w[:, rows].bitcast(E2M1), lhsT_scale=wb_s[:, rows],
+                    rhs=hid_w[:].bitcast(E5M2), rhs_scale=hid_s[:], start=True, stop=True,
+                )
+                nc.tensor.matmul_mx(
+                    out=bank[:, 1, :],
+                    lhsT=wc_w[:, rows].bitcast(E5M2), lhsT_scale=wc_s[:, rows],
+                    rhs=hid_w[:].bitcast(E5M2), rhs_scale=hid_s[:], start=True, stop=True,
+                )
+                nc.vector.tensor_reduce(
+                    out=m0[nh][:, HALF * h : HALF * (h + 1)],
+                    in_=bank[:].rearrange("p a j -> p j a"),
+                    axis=mybir.AxisListType.X, op=ALU.max,
+                )
+
+        for nh in range(2):
+            res = tile("res%d" % nh, J, F32)
+            for h in range(2):
+                cols = slice(HALF * h, HALF * (h + 1))
+                partner = tile("partner%d%d" % (nh, h), HALF, F32)
+                nc.scalar.activation(
+                    out=partner[:], in_=m0[nh][:].indirect(half_of(list3, h)),
+                    func=ACT.Copy, scale=so_t[:, nh : nh + 1],
+                )
+                nc.vector.tensor_tensor(out=res[:, cols], in0=m0[nh][:, cols], in1=partner[:], op=ALU.subtract)
+                if nh == 1:
+                    nc.sync.dma_start(out=out[P * nh : P * (nh + 1), cols], in_=res[:, cols])
+            if nh == 0:
+                nc.sync.dma_start(out=out[P * nh : P * (nh + 1), :], in_=res[:])

@@ -49,18 +49,18 @@ def tile_list_outcomeneighbours_twotab_kernel(
                     in_=src[0, 4 * q : 4 * q + 4, :].bitcast(I32),
                 )
 
-        def load_scale_pairs(queue, first, src):
+        def load_scale_pairs(queue, dst, first, src):
             width = src.shape[2]
             by_quadrant = src[0].rearrange("(b e r) c -> e r b c", b=2, e=2)
             for e in range(2):
                 queue.dma_start(
-                    out=planes[32 * e : 32 * e + 4, :, first : first + width].bitcast(I32),
+                    out=dst[32 * e : 32 * e + 4, :, first : first + width].bitcast(I32),
                     in_=by_quadrant[e].bitcast(I32),
                 )
 
-        def lift_upper_quadrants(width):
+        def lift_upper_quadrants(dst):
             nc.vector.tensor_copy(
-                out=planes[64:128, 0, 0:width].bitcast(I32), in_=planes[0:64, 1, 0:width].bitcast(I32)
+                out=dst[64:128, 0, :].bitcast(I32), in_=dst[0:64, 1, :].bitcast(I32)
             )
 
         def fp8_words(src):
@@ -73,23 +73,27 @@ def tile_list_outcomeneighbours_twotab_kernel(
         xo_w, xo_s = tile("xo_w", TABLE, U32), tile("xo_s", TABLE, U8)
         w_w, w2_w = tile("w_w", R, U32), tile("w2_w", R, U16)
         planes = sb.tile([P, 2, 2 * R], U8, name="planes", align_bytes=64)
+        planes2 = sb.tile([P, 2, 2 * N], U8, name="planes2", align_bytes=64)
         so_t = tile("so_t", 2, F32)
 
-        nc.vector.memset(planes[0:64, :, 0:R].bitcast(I32), 0)
+        nc.gpsimd.memset(planes[0:64, :, 0:R].bitcast(I32), 0)
         nc.vector.memset(planes[0:64, :, R : 2 * R].bitcast(I32), 0)
         nc.vector.memset(xt_s[:].bitcast(I32), 0)
-        nc.vector.memset(xo_s[:].bitcast(I32), 0)
+        nc.gpsimd.memset(xo_s[:].bitcast(I32), 0)
+        nc.vector.memset(planes2[0:64, :, :].bitcast(I32), 0)
 
         load_words(nc.gpsimd, w_w, fp8_words(w_words))
-        load_words(nc.gpsimd, xo_w, fp8_words(xo_words))
         load_words(nc.gpsimd, w2_w, w2_words[0])
         nc.sync.dma_start(list1[:], offs)
         load_words(nc.sync, xt_w, xt_words[0])
         nc.sync.dma_start(list2[:], offs2)
-        load_scale_pairs(nc.sync, 0, w_scales)
-        load_scale_pairs(nc.sync, R, w2_scales)
+        load_scale_pairs(nc.sync, planes, 0, w_scales)
+        load_scale_pairs(nc.sync, planes, R, w2_scales)
+        load_words(nc.sync, xo_w, fp8_words(xo_words))
         load_scales(nc.sync, xt_s, xt_scales)
         load_scales(nc.sync, xo_s, xo_scales)
+        load_scale_pairs(nc.sync, planes2, 0, wb_scales)
+        load_scale_pairs(nc.sync, planes2, N, wc_scales)
         nc.sync.dma_start(list3[:], offs3)
         with nc.allow_non_contiguous_dma(reason="one weight a partition"):
             nc.gpsimd.dma_start(out=so_t[:], in_=so.rearrange("(t p) o -> p (t o)", p=P))
@@ -109,20 +113,18 @@ def tile_list_outcomeneighbours_twotab_kernel(
         def half_of(lst, h):
             return lst[:, 8 * h : 8 * h + 8]
 
-        lift_upper_quadrants(2 * R)
+        lift_upper_quadrants(planes)
         g_xt_w = gathered("g_xt_w", xt_w, list1[:], J, U16)
         w_wd = dealt(nc.scalar.copy, tile("w_wd", R, U32)[:], w_w[:])
-        w2_wd = dealt(nc.scalar.copy, w_w[:, N : 2 * N].bitcast(U16), w2_w[:])
+        w2_wd = dealt(nc.scalar.copy, tile("w2_wd", R, U16)[:], w2_w[:])
         w_sd = dealt(nc.vector.tensor_copy, tile("w_sd", R, U8)[:], planes[:, 0, 0:R])
         w2_sd = dealt(nc.vector.tensor_copy, tile("w2_sd", R, U8)[:], planes[:, 0, R : 2 * R])
         g_xo_w = [gathered("g_xo_w%d" % h, xo_w, half_of(list2, h), HALF, U32) for h in range(2)]
         g_xt_s = [gathered("g_xt_s%d" % h, xt_s, half_of(list1, h), HALF, U8) for h in range(2)]
         g_xo_s = [gathered("g_xo_s%d" % h, xo_s, half_of(list2, h), HALF, U8) for h in range(2)]
 
-        wc_w, wb_w = w_w[:, 0:N], w2_w[:, 0:N]
-        wb_s, wc_s = planes[:, 0, 0:N], planes[:, 0, N : 2 * N]
-        load_scale_pairs(nc.sync, 0, wb_scales)
-        load_scale_pairs(nc.sync, N, wc_scales)
+        wc_w, wb_w = w_w[:, 0:N], w_w[:, N : N + N // 2].bitcast(U16)
+        wb_s, wc_s = planes2[:, 0, 0:N], planes2[:, 0, N : 2 * N]
         load_words(nc.sync, wc_w, fp8_words(wc_words))
         load_words(nc.sync, wb_w, wb_words[0])
 
@@ -159,7 +161,7 @@ def tile_list_outcomeneighbours_twotab_kernel(
                 )
             b_ps.append(bank)
 
-        lift_upper_quadrants(2 * N)
+        lift_upper_quadrants(planes2)
         m0 = [tile("m0_%d" % nh, J, F32) for nh in range(2)]
         for h in range(2):
             hid = tile("hid%d" % h, PACK * HALF, BF16)

from contextlib import ExitStack

import concourse.mybir as mybir

FLOPS = 402653184

F32 = mybir.dt.float32
BF16 = mybir.dt.bfloat16
I32 = mybir.dt.int32
U32 = mybir.dt.uint32
U16 = mybir.dt.uint16
U8 = mybir.dt.uint8
E4M3 = mybir.dt.float8_e4m3fn_x4
E5M2 = mybir.dt.float8_e5m2_x4
E2M1 = mybir.dt.float4_e2m1fn_x4
ACT = mybir.ActivationFunctionType
ALU = mybir.AluOpType

P = 128
PACK = 4
TABLE = 1024
J = 256
R = 512
N = 256
HALF = 128
QUARTER = 64
LIST_ROWS = 16


def tile_list_outcomeneighbours_twotab_kernel(
    tc, xt_words, xt_scales, w_words, w_scales, xo_words, xo_scales, w2_words, w2_scales,
    wb_words, wb_scales, wc_words, wc_scales, so, offs, offs2, offs3, out,
):
    nc = tc.nc
    with ExitStack() as ctx:
        sb = ctx.enter_context(tc.tile_pool(name="sb", bufs=1))
        ps = ctx.enter_context(tc.psum_pool(name="ps", bufs=1))

        def tile(name, width, dtype):
            return sb.tile([P, width], dtype, name=name, align_bytes=64)

        def load_words(queue, dst, src):
            queue.dma_start(out=dst[:].bitcast(I32), in_=src.bitcast(I32))

        def load_scales(queue, dst, src):
            for q in range(4):
                queue.dma_start(
                    out=dst[32 * q : 32 * q + 4, :].bitcast(I32),
                    in_=src[0, 4 * q : 4 * q + 4, :].bitcast(I32),
                )

        def load_scale_pairs(queue, dst, first, src):
            width = src.shape[2]
            by_quadrant = src[0].rearrange("(b e r) c -> e r b c", b=2, e=2)
            for e in range(2):
                queue.dma_start(
                    out=dst[32 * e : 32 * e + 4, :, first : first + width].bitcast(I32),
                    in_=by_quadrant[e].bitcast(I32),
                )

        def lift_upper_quadrants(dst):
            nc.vector.tensor_copy(
                out=dst[64:128, 0, :].bitcast(I32), in_=dst[0:64, 1, :].bitcast(I32)
            )

        def fp8_words(src):
            return src[0].rearrange("p n t -> p (n t)")

        list1 = sb.tile([P, J // LIST_ROWS], U16, name="list1")
        list2 = sb.tile([P, J // LIST_ROWS], U16, name="list2")
        list3 = sb.tile([P, J // LIST_ROWS], U16, name="list3")
        xt_w, xt_s = tile("xt_w", TABLE, U16), tile("xt_s", TABLE, U8)
        xo_w, xo_s = tile("xo_w", TABLE, U32), tile("xo_s", TABLE, U8)
        w_w, w2_w = tile("w_w", R, U32), tile("w2_w", R, U16)
        planes = sb.tile([P, 2, 2 * R], U8, name="planes", align_bytes=64)
        planes2 = sb.tile([P, 2, 2 * N], U8, name="planes2", align_bytes=64)
        so_t = tile("so_t", 2, F32)

        nc.gpsimd.memset(planes[0:64, :, 0:R].bitcast(I32), 0)
        nc.vector.memset(planes[0:64, :, R : 2 * R].bitcast(I32), 0)
        nc.vector.memset(xt_s[:].bitcast(I32), 0)
        nc.gpsimd.memset(xo_s[:].bitcast(I32), 0)
        nc.vector.memset(planes2[0:64, :, :].bitcast(I32), 0)

        load_words(nc.gpsimd, w_w, fp8_words(w_words))
        load_words(nc.gpsimd, w2_w, w2_words[0])
        nc.sync.dma_start(list1[:], offs)
        load_words(nc.sync, xt_w, xt_words[0])
        nc.sync.dma_start(list2[:], offs2)
        load_scale_pairs(nc.sync, planes, 0, w_scales)
        load_scale_pairs(nc.sync, planes, R, w2_scales)
        load_words(nc.sync, xo_w, fp8_words(xo_words))
        load_scales(nc.sync, xt_s, xt_scales)
        load_scales(nc.sync, xo_s, xo_scales)
        load_scale_pairs(nc.sync, planes2, 0, wb_scales)
        load_scale_pairs(nc.sync, planes2, N, wc_scales)
        nc.sync.dma_start(list3[:], offs3)
        with nc.allow_non_contiguous_dma(reason="one weight a partition"):
            nc.gpsimd.dma_start(out=so_t[:], in_=so.rearrange("(t p) o -> p (t o)", p=P))

        def dealt(copy, dst, src):
            copy(
                out=dst.rearrange("p (t m) -> p m t", t=PACK),
                in_=src.rearrange("p (m t) -> p m t", t=PACK),
            )
            return dst

        def gathered(name, table, offsets, width, dtype):
            dst = tile(name, width, dtype)
            nc.vector.tensor_copy(dst[:], table[:].indirect(offsets))
            return dst

        def half_of(lst, h):
            return lst[:, 8 * h : 8 * h + 8]

        lift_upper_quadrants(planes)
        g_xt_w = gathered("g_xt_w", xt_w, list1[:], J, U16)
        w_wd = dealt(nc.scalar.copy, tile("w_wd", R, U32)[:], w_w[:])
        w2_wd = dealt(nc.scalar.copy, tile("w2_wd", R, U16)[:], w2_w[:])
        w_sd = dealt(nc.vector.tensor_copy, tile("w_sd", R, U8)[:], planes[:, 0, 0:R])
        w2_sd = dealt(nc.vector.tensor_copy, tile("w2_sd", R, U8)[:], planes[:, 0, R : 2 * R])
        g_xo_w = [gathered("g_xo_w%d" % h, xo_w, half_of(list2, h), HALF, U32) for h in range(2)]
        g_xt_s = [gathered("g_xt_s%d" % h, xt_s, half_of(list1, h), HALF, U8) for h in range(2)]
        g_xo_s = [gathered("g_xo_s%d" % h, xo_s, half_of(list2, h), HALF, U8) for h in range(2)]

        wc_w, wb_w = w_w[:, 0:N], w_w[:, N : N + N // 2].bitcast(U16)
        wb_s, wc_s = planes2[:, 0, 0:N], planes2[:, 0, N : 2 * N]
        load_words(nc.sync, wc_w, fp8_words(wc_words))
        load_words(nc.sync, wb_w, wb_words[0])

        a_sb = []
        for h in range(2):
            bank = ps.tile([P, PACK, HALF], F32, name="a_ps%d" % h)
            cols = slice(HALF * h, HALF * (h + 1))
            for t in range(PACK):
                rows = slice(P * t, P * (t + 1))
                nc.tensor.matmul_mx(
                    out=bank[:, t, :],
                    lhsT=w_wd[:, rows].bitcast(E4M3), lhsT_scale=w_sd[:, rows],
                    rhs=g_xt_w[:, cols].bitcast(E2M1), rhs_scale=g_xt_s[h][:],
                    start=True, stop=True,
                )
            a_h = tile("a_sb%d" % h, PACK * HALF, F32)
            nc.scalar.activation(
                out=a_h[:].rearrange("p (j t) -> p j t", t=PACK),
                in_=bank[:].rearrange("p t j -> p j t"),
                func=ACT.Copy,
            )
            a_sb.append(a_h)

        b_ps = []
        for h in range(2):
            bank = ps.tile([P, PACK, HALF], F32, name="b_ps%d" % h)
            for t in range(PACK):
                rows = slice(P * t, P * (t + 1))
                nc.tensor.matmul_mx(
                    out=bank[:, t, :],
                    lhsT=w2_wd[:, rows].bitcast(E2M1), lhsT_scale=w2_sd[:, rows],
                    rhs=g_xo_w[h][:].bitcast(E4M3), rhs_scale=g_xo_s[h][:],
                    start=True, stop=True,
                )
            b_ps.append(bank)

        lift_upper_quadrants(planes2)
        m0 = [tile("m0_%d" % nh, J, F32) for nh in range(2)]
        for h in range(2):
            hid = tile("hid%d" % h, PACK * HALF, BF16)
            for u in range(2):
                span = slice(PACK * QUARTER * u, PACK * QUARTER * (u + 1))
                diff = tile("diff%d%d" % (h, u), PACK * QUARTER, F32)
                nc.vector.tensor_tensor(
                    out=diff[:].rearrange("p (j t) -> p j t", t=PACK),
                    in0=a_sb[h][:, span].rearrange("p (j t) -> p j t", t=PACK),
                    in1=b_ps[h][:, :, QUARTER * u : QUARTER * (u + 1)].rearrange("p t j -> p j t"),
                    op=ALU.subtract,
                )
                nc.scalar.activation(out=hid[:, span], in_=diff[:], func=ACT.Abs)
            hid_w, hid_s = tile("hid_w%d" % h, HALF, U32), tile("hid_s%d" % h, HALF, U8)
            nc.vector.quantize_mx(out=hid_w[:].bitcast(E5M2), scales=hid_s[:], in_=hid[:])
            for nh in range(2):
                rows = slice(P * nh, P * (nh + 1))
                bank = ps.tile([P, 2, HALF], F32, name="pq_ps%d%d" % (h, nh))
                nc.tensor.matmul_mx(
                    out=bank[:, 0, :],
                    lhsT=wb_w[:, rows].bitcast(E2M1), lhsT_scale=wb_s[:, rows],
                    rhs=hid_w[:].bitcast(E5M2), rhs_scale=hid_s[:], start=True, stop=True,
                )
                nc.tensor.matmul_mx(
                    out=bank[:, 1, :],
                    lhsT=wc_w[:, rows].bitcast(E5M2), lhsT_scale=wc_s[:, rows],
                    rhs=hid_w[:].bitcast(E5M2), rhs_scale=hid_s[:], start=True, stop=True,
                )
                nc.vector.tensor_reduce(
                    out=m0[nh][:, HALF * h : HALF * (h + 1)],
                    in_=bank[:].rearrange("p a j -> p j a"),
                    axis=mybir.AxisListType.X, op=ALU.max,
                )

        for nh in range(2):
            res = tile("res%d" % nh, J, F32)
            for h in range(2):
                cols = slice(HALF * h, HALF * (h + 1))
                partner = tile("partner%d%d" % (nh, h), HALF, F32)
                nc.scalar.activation(
                    out=partner[:], in_=m0[nh][:].indirect(half_of(list3, h)),
                    func=ACT.Copy, scale=so_t[:, nh : nh + 1],
                )
                nc.vector.tensor_tensor(out=res[:, cols], in0=m0[nh][:, cols], in1=partner[:], op=ALU.subtract)
                if nh == 1:
                    nc.sync.dma_start(out=out[P * nh : P * (nh + 1), cols], in_=res[:, cols])
            if nh == 0:
                nc.sync.dma_start(out=out[P * nh : P * (nh + 1), :], in_=res[:])
